import numpy as np
import ml_dtypes


def mxq(x, axis, fmt="e4m3"):
    dtype, down = {"e4m3": (ml_dtypes.float8_e4m3fn, 7), "e5m2": (ml_dtypes.float8_e5m2, 14)}[fmt]
    v = np.moveaxis(np.asarray(x, np.float32).astype(ml_dtypes.bfloat16).astype(np.float64), axis, -1)
    blocks = v.reshape(v.shape[:-1] + (-1, 32))
    amax = np.abs(blocks).max(-1, keepdims=True)
    byte = np.maximum(np.where(amax > 0, np.frexp(amax)[1] - 1 + 127, 0) - down, 1)
    scale = np.exp2(byte - 127.0)
    codes = (blocks / scale).astype(np.float32).astype(dtype).astype(np.float64)
    return np.moveaxis((codes * scale).reshape(v.shape), -1, axis)


WIDE = False


def mx_kscale(k, group=512):
    if not WIDE:
        return np.ones(k)
    levels = np.array([18, -18])
    if group != 512:
        return np.exp2(np.random.permutation(np.resize(levels, k // group))).repeat(group)
    if k % 512:
        return np.exp2(np.random.permutation(np.resize(levels, k // 32))).repeat(32)
    a = np.empty((k // 512, 16))
    for p in range(k // 512):
        a[p, :8] = np.random.permutation(np.resize(levels, 8))
        for g in range(8):
            far = levels[np.abs(levels - a[p, g]) >= 10]
            a[p, g + 8] = far[np.random.randint(len(far))]
    return np.exp2(a.ravel()).repeat(32)


def f64(x):
    return np.asarray(x).astype(np.float64)


def sigmoid(v):
    return 1.0 / (1.0 + np.exp(-v))


G, D, M, O, N = 4, 128, 128, 128, 512


def sgn(shape):
    return np.random.uniform(0.5, 2.0, shape) * np.where(np.random.standard_normal(shape) < 0, -1.0, 1.0)


def setup_inputs():
    n = np.random.standard_normal
    s_d = mx_kscale(D, 0)
    s_m = mx_kscale(M, 0)
    return {
        "x": (n((G, D, N)) * s_d[:, None]).astype(np.float32),
        "w1": (n((G, D, M)) / np.sqrt(D) / s_d[:, None]).astype(np.float32),
        "w2": (n((G, D, M)) / np.sqrt(D) / s_d[:, None]).astype(np.float32),
        "st": (np.random.uniform(4.0, 16.0, (G, M, 1))).astype(np.float32),
        "gb": (0.5 * n((G, M, 1))).astype(np.float32),
        "hs": (sgn((G, M, 1)) * s_m[:, None]).astype(np.float32),
        "wo2": (n((G, M, O)) / np.sqrt(M) / s_m[:, None]).astype(np.float32),
        "res": (0.5 * n((G, O, N))).astype(np.float32),
    }


def reference(x, w1, w2, st, gb, hs, wo2, res):
    w1q = mxq(f64(w1), 1, "e4m3")
    xq = mxq(f64(x), 1, "e4m3")
    z1 = w1q.transpose(0, 2, 1) @ xq
    w2q = mxq(f64(w2), 1, "e4m3")
    z2 = w2q.transpose(0, 2, 1) @ xq
    mu = np.mean(z1 * z2, axis=-1, keepdims=True)
    gt = sigmoid(mu * f64(st) + f64(gb))
    h = z1 * gt
    hh = h * f64(hs)
    wo2q = mxq(f64(wo2), 1, "e4m3")
    hhq = mxq(hh, 1, "e4m3")
    y0 = wo2q.transpose(0, 2, 1) @ hhq
    y = y0 + f64(res)
    return y

@@ -1,0 +1,161 @@
+from contextlib import ExitStack
+
+import concourse.mybir as mybir
+
+G, D, M, O, N = 4, 128, 128, 128, 512
+FLOPS = 3 * 2 * G * D * M * N
+
+F32 = mybir.dt.float32
+BF16 = mybir.dt.bfloat16
+U32 = mybir.dt.uint32
+U8 = mybir.dt.uint8
+FP8X4 = mybir.dt.float8_e4m3fn_x4
+ACT = mybir.ActivationFunctionType
+ALU = mybir.AluOpType
+
+P = 128
+PACK = 4
+ROWS = 32
+RUN = 4
+X_SPLIT = 336
+H_SPLIT = 336
+
+
+def interleave(copy, grouped, rows, lo, hi):
+    copy(
+        out=grouped[:, lo:hi, :].rearrange("p (c i) j -> p c j i", i=RUN),
+        in_=rows[:, :, lo:hi].rearrange("p j (c i) -> p c j i", i=RUN),
+    )
+
+
+def quantize(nc, codes, scales, grouped):
+    nc.vector.quantize_mx(
+        out=codes[:].bitcast(FP8X4),
+        scales=scales[:],
+        in_=grouped[:].rearrange("p w j -> p (w j)"),
+    )
+
+
+def product(nc, bank, g, w_codes, w_scales, a_codes, a_scales):
+    rows = slice(ROWS * g, ROWS * (g + 1))
+    nc.tensor.matmul_mx(
+        out=bank[:],
+        lhsT=w_codes[rows, :].bitcast(FP8X4),
+        lhsT_scale=w_scales[rows, :],
+        rhs=a_codes[rows, :].bitcast(FP8X4),
+        rhs_scale=a_scales[rows, :],
+        start=True,
+        stop=True,
+    )
+
+
+def tile_rows_frowgate_kernel(tc, x, w1, w2, st, gb, hs, wo2, res, out):
+    nc = tc.nc
+    with ExitStack() as ctx:
+        sb = ctx.enter_context(tc.tile_pool(name="sb", bufs=1))
+        ps = ctx.enter_context(tc.psum_pool(name="ps", bufs=1))
+        ctx.enter_context(tc.manual_schedule())
+
+        def operand(name, width, raw_dtype):
+            raw = sb.tile([P, PACK, width], raw_dtype, name=name + "_raw", align_bytes=64)
+            grouped = sb.tile([P, width, PACK], BF16, name=name + "_grouped", align_bytes=64)
+            codes = sb.tile([P, width], U32, name=name + "_codes", align_bytes=64)
+            scales = sb.tile([P, width], U8, name=name + "_scales", align_bytes=64)
+            return raw, grouped, codes, scales
+
+        x_raw, x_grp, x_codes, x_scales = operand("x", N, F32)
+        w1_raw, w1_grp, w1_codes, w1_scales = operand("w1", M, F32)
+        w2_raw, w2_grp, w2_codes, w2_scales = operand("w2", M, F32)
+        wo_raw, wo_grp, wo_codes, wo_scales = operand("wo", O, F32)
+        h_raw, h_grp, h_codes, h_scales = operand("h", N, BF16)
+
+        st_sb = sb.tile([P, G], F32, name="st_sb")
+        gb_sb = sb.tile([P, G], F32, name="gb_sb")
+        hs_sb = sb.tile([P, G], F32, name="hs_sb")
+        res_sb = sb.tile([P, G, N], F32, name="res_sb")
+        mu = [sb.tile([P, 1], F32, name="mu%d" % g) for g in range(G)]
+        gt = [sb.tile([P, 1], F32, name="gt%d" % g) for g in range(G)]
+        gs = [sb.tile([P, 1], F32, name="gs%d" % g) for g in range(G)]
+        z1 = [sb.tile([P, N], F32, name="z1_%d" % g) for g in range(G)]
+        prod = [sb.tile([P, N], F32, name="prod%d" % g) for g in range(G)]
+        hh = [sb.tile([P, N], BF16, name="hh%d" % g) for g in range(G)]
+        y = [sb.tile([P, N], F32, name="y%d" % g) for g in range(G)]
+        bank_a = [ps.tile([P, N], F32, name="bank_a%d" % g) for g in range(G)]
+        bank_b = [ps.tile([P, N], F32, name="bank_b%d" % g) for g in range(G)]
+
+        warm_in = sb.tile([P, 1], F32, name="warm_in")
+        warm_out = sb.tile([P, 1], F32, name="warm_out")
+        nc.vector.memset(warm_in[:], 0.0)
+        nc.scalar.activation(out=warm_out[:], in_=warm_in[:], func=ACT.Sigmoid)
+
+        for raw, src in ((x_raw, x), (w1_raw, w1), (w2_raw, w2)):
+            nc.sync.dma_start(out=raw[:], in_=src.rearrange("g (p j) c -> (g p) j c", j=PACK))
+        with nc.allow_non_contiguous_dma(reason="one value a partition"):
+            for col, src in ((st_sb, st), (gb_sb, gb), (hs_sb, hs)):
+                nc.sync.dma_start(out=col[:], in_=src.rearrange("g m o -> m (g o)"))
+        nc.sync.dma_start(out=wo_raw[:], in_=wo2.rearrange("g (p j) c -> (g p) j c", j=PACK))
+        nc.sync.dma_start(out=res_sb[:], in_=res.rearrange("g o n -> o g n"))
+
+        interleave(nc.vector.tensor_copy, x_grp, x_raw, 0, X_SPLIT)
+        interleave(nc.scalar.copy, x_grp, x_raw, X_SPLIT, N)
+        interleave(nc.scalar.copy, w1_grp, w1_raw, 0, M)
+        quantize(nc, x_codes, x_scales, x_grp)
+        interleave(nc.vector.tensor_copy, w2_grp, w2_raw, 0, M)
+        quantize(nc, w1_codes, w1_scales, w1_grp)
+        quantize(nc, w2_codes, w2_scales, w2_grp)
+
+        order = (0, 2, 1, 3)
+        for g in order:
+            product(nc, bank_a[g], g, w1_codes, w1_scales, x_codes, x_scales)
+        for g in order:
+            product(nc, bank_b[g], g, w2_codes, w2_scales, x_codes, x_scales)
+
+        for g in order:
+            nc.scalar.copy(out=z1[g][:], in_=bank_a[g][:])
+            nc.vector.scalar_tensor_tensor(
+                out=prod[g][:], in0=bank_b[g][:], scalar=1.0 / N, in1=z1[g][:],
+                op0=ALU.mult, op1=ALU.mult, accum_out=mu[g][:],
+            )
+
+        def gate(g):
+            nc.scalar.activation(
+                out=gt[g][:], in_=mu[g][:], func=ACT.Sigmoid,
+                scale=st_sb[:, g : g + 1], bias=gb_sb[:, g : g + 1],
+            )
+
+        def move(g):
+            nc.sync.dma_start(out=h_raw[ROWS * g : ROWS * (g + 1), :, :], in_=hh[g][:])
+
+        def scale_on_scalar(g):
+            nc.scalar.activation(out=gs[g][:], in_=gt[g][:], func=ACT.Copy, scale=hs_sb[:, g : g + 1])
+            nc.scalar.activation(out=hh[g][:], in_=z1[g][:], func=ACT.Copy, scale=gs[g][:])
+            move(g)
+
+        def scale_on_vector(g):
+            nc.vector.tensor_scalar(
+                out=hh[g][:], in0=z1[g][:], scalar1=gt[g][:], scalar2=hs_sb[:, g : g + 1],
+                op0=ALU.mult, op1=ALU.mult,
+            )
+            move(g)
+
+        gate(order[0])
+        gate(order[1])
+        scale_on_scalar(order[0])
+        gate(order[2])
+        gate(order[3])
+        scale_on_vector(order[1])
+        scale_on_vector(order[2])
+        scale_on_vector(order[3])
+
+        interleave(nc.vector.tensor_copy, wo_grp, wo_raw, 0, O)
+        quantize(nc, wo_codes, wo_scales, wo_grp)
+
+        interleave(nc.vector.tensor_copy, h_grp, h_raw, 0, H_SPLIT)
+        interleave(nc.scalar.copy, h_grp, h_raw, H_SPLIT, N)
+        quantize(nc, h_codes, h_scales, h_grp)
+
+        for g in order:
+            product(nc, bank_a[g], g, wo_codes, wo_scales, h_codes, h_scales)
+        for g in order:
+            nc.vector.tensor_tensor(out=y[g][:], in0=bank_a[g][:], in1=res_sb[:, g, :], op=ALU.add)
+            nc.sync.dma_start(out=out[g], in_=y[g][:])

@@ -17,8 +17,9 @@ P = 128
 PACK = 4
 ROWS = 32
 RUN = 4
-X_SPLIT = 336
-H_SPLIT = 336
+HALF = N // 2
+X_SPLIT = 384
+H_SPLIT = 352
 
 
 def interleave(copy, grouped, rows, lo, hi):
@@ -28,11 +29,11 @@ def interleave(copy, grouped, rows, lo, hi):
     )
 
 
-def quantize(nc, codes, scales, grouped):
+def quantize(nc, codes, scales, grouped, lo, hi):
     nc.vector.quantize_mx(
-        out=codes[:].bitcast(FP8X4),
-        scales=scales[:],
-        in_=grouped[:].rearrange("p w j -> p (w j)"),
+        out=codes[:, lo:hi].bitcast(FP8X4),
+        scales=scales[:, lo:hi],
+        in_=grouped[:, lo:hi, :].rearrange("p w j -> p (w j)"),
     )
 
 
@@ -69,9 +70,18 @@ def tile_rows_frowgate_kernel(tc, x, w1, w2, st, gb, hs, wo2, res, out):
         wo_raw, wo_grp, wo_codes, wo_scales = operand("wo", O, F32)
         h_raw, h_grp, h_codes, h_scales = operand("h", N, BF16)
 
-        st_sb = sb.tile([P, G], F32, name="st_sb")
-        gb_sb = sb.tile([P, G], F32, name="gb_sb")
-        hs_sb = sb.tile([P, G], F32, name="hs_sb")
+        vec_rows = sb.tile([P, G * ROWS], F32, name="vec_rows", align_bytes=64)
+        vec_cols = sb.tile([P, G * ROWS], F32, name="vec_cols", align_bytes=64)
+
+        def st_col(g):
+            return vec_cols[:, ROWS * g : ROWS * g + 1]
+
+        def gb_col(g):
+            return vec_cols[:, ROWS * g + 1 : ROWS * g + 2]
+
+        def hs_col(g):
+            return vec_cols[:, ROWS * g + 2 : ROWS * g + 3]
+
         res_sb = sb.tile([P, G, N], F32, name="res_sb")
         mu = [sb.tile([P, 1], F32, name="mu%d" % g) for g in range(G)]
         gt = [sb.tile([P, 1], F32, name="gt%d" % g) for g in range(G)]
@@ -86,23 +96,29 @@ def tile_rows_frowgate_kernel(tc, x, w1, w2, st, gb, hs, wo2, res, out):
         warm_in = sb.tile([P, 1], F32, name="warm_in")
         warm_out = sb.tile([P, 1], F32, name="warm_out")
         nc.vector.memset(warm_in[:], 0.0)
+        nc.vector.memset(vec_rows[:], 0.0)
         nc.scalar.activation(out=warm_out[:], in_=warm_in[:], func=ACT.Sigmoid)
 
         for raw, src in ((x_raw, x), (w1_raw, w1), (w2_raw, w2)):
             nc.sync.dma_start(out=raw[:], in_=src.rearrange("g (p j) c -> (g p) j c", j=PACK))
-        with nc.allow_non_contiguous_dma(reason="one value a partition"):
-            for col, src in ((st_sb, st), (gb_sb, gb), (hs_sb, hs)):
-                nc.sync.dma_start(out=col[:], in_=src.rearrange("g m o -> m (g o)"))
+        for r, src in enumerate((st, gb, hs)):
+            nc.sync.dma_start(
+                out=vec_rows[r:P:ROWS, :].rearrange("q (g i) -> q g i", g=G),
+                in_=src.rearrange("g (q i) o -> q g (i o)", i=ROWS),
+            )
         nc.sync.dma_start(out=wo_raw[:], in_=wo2.rearrange("g (p j) c -> (g p) j c", j=PACK))
         nc.sync.dma_start(out=res_sb[:], in_=res.rearrange("g o n -> o g n"))
 
-        interleave(nc.vector.tensor_copy, x_grp, x_raw, 0, X_SPLIT)
+        interleave(nc.vector.tensor_copy, x_grp, x_raw, 0, HALF)
+        interleave(nc.vector.tensor_copy, x_grp, x_raw, HALF, X_SPLIT)
         interleave(nc.scalar.copy, x_grp, x_raw, X_SPLIT, N)
         interleave(nc.scalar.copy, w1_grp, w1_raw, 0, M)
-        quantize(nc, x_codes, x_scales, x_grp)
-        interleave(nc.vector.tensor_copy, w2_grp, w2_raw, 0, M)
-        quantize(nc, w1_codes, w1_scales, w1_grp)
-        quantize(nc, w2_codes, w2_scales, w2_grp)
+        interleave(nc.scalar.copy, w2_grp, w2_raw, 0, M)
+        quantize(nc, x_codes, x_scales, x_grp, 0, HALF)
+        quantize(nc, x_codes, x_scales, x_grp, HALF, N)
+        quantize(nc, w1_codes, w1_scales, w1_grp, 0, M)
+        quantize(nc, w2_codes, w2_scales, w2_grp, 0, M)
+        nc.vector.transpose(out=vec_cols[:], in_=vec_rows[:])
 
         order = (0, 2, 1, 3)
         for g in order:
@@ -120,42 +136,46 @@ def tile_rows_frowgate_kernel(tc, x, w1, w2, st, gb, hs, wo2, res, out):
         def gate(g):
             nc.scalar.activation(
                 out=gt[g][:], in_=mu[g][:], func=ACT.Sigmoid,
-                scale=st_sb[:, g : g + 1], bias=gb_sb[:, g : g + 1],
+                scale=st_col(g), bias=gb_col(g),
             )
 
-        def move(g):
-            nc.sync.dma_start(out=h_raw[ROWS * g : ROWS * (g + 1), :, :], in_=hh[g][:])
+        def move(g, cols):
+            nc.sync.dma_start(out=h_raw[ROWS * g : ROWS * (g + 1), :, cols], in_=hh[g][:, cols])
 
         def scale_on_scalar(g):
-            nc.scalar.activation(out=gs[g][:], in_=gt[g][:], func=ACT.Copy, scale=hs_sb[:, g : g + 1])
+            nc.scalar.activation(out=gs[g][:], in_=gt[g][:], func=ACT.Copy, scale=hs_col(g))
             nc.scalar.activation(out=hh[g][:], in_=z1[g][:], func=ACT.Copy, scale=gs[g][:])
-            move(g)
+            move(g, slice(0, N))
 
-        def scale_on_vector(g):
+        def scale_on_vector(g, cols):
             nc.vector.tensor_scalar(
-                out=hh[g][:], in0=z1[g][:], scalar1=gt[g][:], scalar2=hs_sb[:, g : g + 1],
+                out=hh[g][:, cols], in0=z1[g][:, cols], scalar1=gt[g][:], scalar2=hs_col(g),
                 op0=ALU.mult, op1=ALU.mult,
             )
-            move(g)
+            move(g, cols)
 
         gate(order[0])
         gate(order[1])
         scale_on_scalar(order[0])
         gate(order[2])
         gate(order[3])
-        scale_on_vector(order[1])
-        scale_on_vector(order[2])
-        scale_on_vector(order[3])
+        scale_on_vector(order[1], slice(0, N))
+        scale_on_vector(order[2], slice(0, N))
+        scale_on_vector(order[3], slice(0, HALF))
+        scale_on_vector(order[3], slice(HALF, N))
 
         interleave(nc.vector.tensor_copy, wo_grp, wo_raw, 0, O)
-        quantize(nc, wo_codes, wo_scales, wo_grp)
+        quantize(nc, wo_codes, wo_scales, wo_grp, 0, O)
 
-        interleave(nc.vector.tensor_copy, h_grp, h_raw, 0, H_SPLIT)
+        interleave(nc.vector.tensor_copy, h_grp, h_raw, 0, HALF)
+        interleave(nc.vector.tensor_copy, h_grp, h_raw, HALF, H_SPLIT)
         interleave(nc.scalar.copy, h_grp, h_raw, H_SPLIT, N)
-        quantize(nc, h_codes, h_scales, h_grp)
+        quantize(nc, h_codes, h_scales, h_grp, 0, HALF)
+        quantize(nc, h_codes, h_scales, h_grp, HALF, N)
 
         for g in order:
             product(nc, bank_a[g], g, wo_codes, wo_scales, h_codes, h_scales)
         for g in order:
-            nc.vector.tensor_tensor(out=y[g][:], in0=bank_a[g][:], in1=res_sb[:, g, :], op=ALU.add)
-            nc.sync.dma_start(out=out[g], in_=y[g][:])
+            for cols in (slice(0, HALF), slice(HALF, N)):
+                nc.vector.tensor_tensor(out=y[g][:, cols], in0=bank_a[g][:, cols], in1=res_sb[:, g, cols], op=ALU.add)
+                nc.sync.dma_start(out=out[g][:, cols], in_=y[g][:, cols])

@@ -126,8 +126,10 @@ def tile_rows_frowgate_kernel(tc, x, w1, w2, st, gb, hs, wo2, res, out):
         for g in order:
             product(nc, bank_b[g], g, w2_codes, w2_scales, x_codes, x_scales)
 
-        for g in order:
+        def copy_z1(g):
             nc.scalar.copy(out=z1[g][:], in_=bank_a[g][:])
+
+        def row_mean(g):
             nc.vector.scalar_tensor_tensor(
                 out=prod[g][:], in0=bank_b[g][:], scalar=1.0 / N, in1=z1[g][:],
                 op0=ALU.mult, op1=ALU.mult, accum_out=mu[g][:],
@@ -135,37 +137,50 @@ def tile_rows_frowgate_kernel(tc, x, w1, w2, st, gb, hs, wo2, res, out):
 
         def gate(g):
             nc.scalar.activation(
-                out=gt[g][:], in_=mu[g][:], func=ACT.Sigmoid,
-                scale=st_col(g), bias=gb_col(g),
+                out=gt[g][:], in_=mu[g][:], func=ACT.Sigmoid, scale=st_col(g), bias=gb_col(g),
             )
 
         def move(g, cols):
             nc.sync.dma_start(out=h_raw[ROWS * g : ROWS * (g + 1), :, cols], in_=hh[g][:, cols])
 
-        def scale_on_scalar(g):
-            nc.scalar.activation(out=gs[g][:], in_=gt[g][:], func=ACT.Copy, scale=hs_col(g))
-            nc.scalar.activation(out=hh[g][:], in_=z1[g][:], func=ACT.Copy, scale=gs[g][:])
-            move(g, slice(0, N))
-
-        def scale_on_vector(g, cols):
-            nc.vector.tensor_scalar(
+        def scale(engine, g, cols):
+            engine.tensor_scalar(
                 out=hh[g][:, cols], in0=z1[g][:, cols], scalar1=gt[g][:], scalar2=hs_col(g),
                 op0=ALU.mult, op1=ALU.mult,
             )
             move(g, cols)
 
-        gate(order[0])
-        gate(order[1])
-        scale_on_scalar(order[0])
-        gate(order[2])
-        gate(order[3])
-        scale_on_vector(order[1], slice(0, N))
-        scale_on_vector(order[2], slice(0, N))
-        scale_on_vector(order[3], slice(0, HALF))
-        scale_on_vector(order[3], slice(HALF, N))
+        first, second, third, last = order
+        for g in (first, second, third):
+            copy_z1(g)
+            row_mean(g)
+        gate(first)
+        scale(nc.gpsimd, first, slice(0, HALF))
+        scale(nc.gpsimd, first, slice(HALF, N))
+        copy_z1(last)
+        row_mean(last)
+        gate(second)
+        nc.scalar.activation(out=gs[second][:], in_=gt[second][:], func=ACT.Copy, scale=hs_col(second))
+        gate(third)
+        nc.scalar.activation(out=hh[second][:], in_=z1[second][:], func=ACT.Copy, scale=gs[second][:])
+        move(second, slice(0, N))
+        gate(last)
+        scale(nc.vector, third, slice(0, N))
+        scale(nc.vector, last, slice(0, HALF))
+        scale(nc.vector, last, slice(HALF, N))
 
-        interleave(nc.vector.tensor_copy, wo_grp, wo_raw, 0, O)
+        interleave(nc.scalar.copy, wo_grp, wo_raw, 0, O)
+
+        e_grp = sb.tile([ROWS, N, PACK], BF16, name="e_grouped", align_bytes=64)
+        e_codes = sb.tile([ROWS, N], U32, name="e_codes", align_bytes=64)
+        e_scales = sb.tile([ROWS, N], U8, name="e_scales", align_bytes=64)
+        interleave(nc.vector.tensor_copy, e_grp, h_raw[0:ROWS], 0, HALF)
+        interleave(nc.vector.tensor_copy, e_grp, h_raw[0:ROWS], HALF, H_SPLIT)
+        interleave(nc.scalar.copy, e_grp, h_raw[0:ROWS], H_SPLIT, N)
         quantize(nc, wo_codes, wo_scales, wo_grp, 0, O)
+        for lo in range(0, N, 128):
+            quantize(nc, e_codes, e_scales, e_grp, lo, lo + 128)
+        product(nc, bank_a[first], first, wo_codes, wo_scales, e_codes, e_scales)
 
         interleave(nc.vector.tensor_copy, h_grp, h_raw, 0, HALF)
         interleave(nc.vector.tensor_copy, h_grp, h_raw, HALF, H_SPLIT)
@@ -173,7 +188,7 @@ def tile_rows_frowgate_kernel(tc, x, w1, w2, st, gb, hs, wo2, res, out):
         quantize(nc, h_codes, h_scales, h_grp, 0, HALF)
         quantize(nc, h_codes, h_scales, h_grp, HALF, N)
 
-        for g in order:
+        for g in order[1:]:
             product(nc, bank_a[g], g, wo_codes, wo_scales, h_codes, h_scales)
         for g in order:
             for cols in (slice(0, HALF), slice(HALF, N)):

from contextlib import ExitStack

import concourse.mybir as mybir

G, D, M, O, N = 4, 128, 128, 128, 512
FLOPS = 3 * 2 * G * D * M * N

F32 = mybir.dt.float32
BF16 = mybir.dt.bfloat16
U32 = mybir.dt.uint32
U8 = mybir.dt.uint8
FP8X4 = mybir.dt.float8_e4m3fn_x4
ACT = mybir.ActivationFunctionType
ALU = mybir.AluOpType

P = 128
PACK = 4
ROWS = 32
RUN = 4
HALF = N // 2
X_SPLIT = 384
H_SPLIT = 352


def interleave(copy, grouped, rows, lo, hi):
    copy(
        out=grouped[:, lo:hi, :].rearrange("p (c i) j -> p c j i", i=RUN),
        in_=rows[:, :, lo:hi].rearrange("p j (c i) -> p c j i", i=RUN),
    )


def quantize(nc, codes, scales, grouped, lo, hi):
    nc.vector.quantize_mx(
        out=codes[:, lo:hi].bitcast(FP8X4),
        scales=scales[:, lo:hi],
        in_=grouped[:, lo:hi, :].rearrange("p w j -> p (w j)"),
    )


def product(nc, bank, g, w_codes, w_scales, a_codes, a_scales):
    rows = slice(ROWS * g, ROWS * (g + 1))
    nc.tensor.matmul_mx(
        out=bank[:],
        lhsT=w_codes[rows, :].bitcast(FP8X4),
        lhsT_scale=w_scales[rows, :],
        rhs=a_codes[rows, :].bitcast(FP8X4),
        rhs_scale=a_scales[rows, :],
        start=True,
        stop=True,
    )


def tile_rows_frowgate_kernel(tc, x, w1, w2, st, gb, hs, wo2, res, out):
    nc = tc.nc
    with ExitStack() as ctx:
        sb = ctx.enter_context(tc.tile_pool(name="sb", bufs=1))
        ps = ctx.enter_context(tc.psum_pool(name="ps", bufs=1))
        ctx.enter_context(tc.manual_schedule())

        def operand(name, width, raw_dtype):
            raw = sb.tile([P, PACK, width], raw_dtype, name=name + "_raw", align_bytes=64)
            grouped = sb.tile([P, width, PACK], BF16, name=name + "_grouped", align_bytes=64)
            codes = sb.tile([P, width], U32, name=name + "_codes", align_bytes=64)
            scales = sb.tile([P, width], U8, name=name + "_scales", align_bytes=64)
            return raw, grouped, codes, scales

        x_raw, x_grp, x_codes, x_scales = operand("x", N, F32)
        w1_raw, w1_grp, w1_codes, w1_scales = operand("w1", M, F32)
        w2_raw, w2_grp, w2_codes, w2_scales = operand("w2", M, F32)
        wo_raw, wo_grp, wo_codes, wo_scales = operand("wo", O, F32)
        h_raw, h_grp, h_codes, h_scales = operand("h", N, BF16)

        vec_rows = sb.tile([P, G * ROWS], F32, name="vec_rows", align_bytes=64)
        vec_cols = sb.tile([P, G * ROWS], F32, name="vec_cols", align_bytes=64)

        def st_col(g):
            return vec_cols[:, ROWS * g : ROWS * g + 1]

        def gb_col(g):
            return vec_cols[:, ROWS * g + 1 : ROWS * g + 2]

        def hs_col(g):
            return vec_cols[:, ROWS * g + 2 : ROWS * g + 3]

        res_sb = sb.tile([P, G, N], F32, name="res_sb")
        mu = [sb.tile([P, 1], F32, name="mu%d" % g) for g in range(G)]
        gt = [sb.tile([P, 1], F32, name="gt%d" % g) for g in range(G)]
        gs = [sb.tile([P, 1], F32, name="gs%d" % g) for g in range(G)]
        z1 = [sb.tile([P, N], F32, name="z1_%d" % g) for g in range(G)]
        prod = [sb.tile([P, N], F32, name="prod%d" % g) for g in range(G)]
        hh = [sb.tile([P, N], BF16, name="hh%d" % g) for g in range(G)]
        y = [sb.tile([P, N], F32, name="y%d" % g) for g in range(G)]
        bank_a = [ps.tile([P, N], F32, name="bank_a%d" % g) for g in range(G)]
        bank_b = [ps.tile([P, N], F32, name="bank_b%d" % g) for g in range(G)]

        warm_in = sb.tile([P, 1], F32, name="warm_in")
        warm_out = sb.tile([P, 1], F32, name="warm_out")
        nc.vector.memset(warm_in[:], 0.0)
        nc.vector.memset(vec_rows[:], 0.0)
        nc.scalar.activation(out=warm_out[:], in_=warm_in[:], func=ACT.Sigmoid)

        for raw, src in ((x_raw, x), (w1_raw, w1), (w2_raw, w2)):
            nc.sync.dma_start(out=raw[:], in_=src.rearrange("g (p j) c -> (g p) j c", j=PACK))
        for r, src in enumerate((st, gb, hs)):
            nc.sync.dma_start(
                out=vec_rows[r:P:ROWS, :].rearrange("q (g i) -> q g i", g=G),
                in_=src.rearrange("g (q i) o -> q g (i o)", i=ROWS),
            )
        nc.sync.dma_start(out=wo_raw[:], in_=wo2.rearrange("g (p j) c -> (g p) j c", j=PACK))
        nc.sync.dma_start(out=res_sb[:], in_=res.rearrange("g o n -> o g n"))

        interleave(nc.vector.tensor_copy, x_grp, x_raw, 0, HALF)
        interleave(nc.vector.tensor_copy, x_grp, x_raw, HALF, X_SPLIT)
        interleave(nc.scalar.copy, x_grp, x_raw, X_SPLIT, N)
        interleave(nc.scalar.copy, w1_grp, w1_raw, 0, M)
        interleave(nc.scalar.copy, w2_grp, w2_raw, 0, M)
        quantize(nc, x_codes, x_scales, x_grp, 0, HALF)
        quantize(nc, x_codes, x_scales, x_grp, HALF, N)
        quantize(nc, w1_codes, w1_scales, w1_grp, 0, M)
        quantize(nc, w2_codes, w2_scales, w2_grp, 0, M)
        nc.vector.transpose(out=vec_cols[:], in_=vec_rows[:])

        order = (0, 2, 1, 3)
        for g in order:
            product(nc, bank_a[g], g, w1_codes, w1_scales, x_codes, x_scales)
        for g in order:
            product(nc, bank_b[g], g, w2_codes, w2_scales, x_codes, x_scales)

        def copy_z1(g):
            nc.scalar.copy(out=z1[g][:], in_=bank_a[g][:])

        def row_mean(g):
            nc.vector.scalar_tensor_tensor(
                out=prod[g][:], in0=bank_b[g][:], scalar=1.0 / N, in1=z1[g][:],
                op0=ALU.mult, op1=ALU.mult, accum_out=mu[g][:],
            )

        def gate(g):
            nc.scalar.activation(
                out=gt[g][:], in_=mu[g][:], func=ACT.Sigmoid, scale=st_col(g), bias=gb_col(g),
            )

        def move(g, cols):
            nc.sync.dma_start(out=h_raw[ROWS * g : ROWS * (g + 1), :, cols], in_=hh[g][:, cols])

        def scale(engine, g, cols):
            engine.tensor_scalar(
                out=hh[g][:, cols], in0=z1[g][:, cols], scalar1=gt[g][:], scalar2=hs_col(g),
                op0=ALU.mult, op1=ALU.mult,
            )
            move(g, cols)

        first, second, third, last = order
        for g in (first, second, third):
            copy_z1(g)
            row_mean(g)
        gate(first)
        scale(nc.gpsimd, first, slice(0, HALF))
        scale(nc.gpsimd, first, slice(HALF, N))
        copy_z1(last)
        row_mean(last)
        gate(second)
        nc.scalar.activation(out=gs[second][:], in_=gt[second][:], func=ACT.Copy, scale=hs_col(second))
        gate(third)
        nc.scalar.activation(out=hh[second][:], in_=z1[second][:], func=ACT.Copy, scale=gs[second][:])
        move(second, slice(0, N))
        gate(last)
        scale(nc.vector, third, slice(0, N))
        scale(nc.vector, last, slice(0, HALF))
        scale(nc.vector, last, slice(HALF, N))

        interleave(nc.scalar.copy, wo_grp, wo_raw, 0, O)

        e_grp = sb.tile([ROWS, N, PACK], BF16, name="e_grouped", align_bytes=64)
        e_codes = sb.tile([ROWS, N], U32, name="e_codes", align_bytes=64)
        e_scales = sb.tile([ROWS, N], U8, name="e_scales", align_bytes=64)
        interleave(nc.vector.tensor_copy, e_grp, h_raw[0:ROWS], 0, HALF)
        interleave(nc.vector.tensor_copy, e_grp, h_raw[0:ROWS], HALF, H_SPLIT)
        interleave(nc.scalar.copy, e_grp, h_raw[0:ROWS], H_SPLIT, N)
        quantize(nc, wo_codes, wo_scales, wo_grp, 0, O)
        for lo in range(0, N, 128):
            quantize(nc, e_codes, e_scales, e_grp, lo, lo + 128)
        product(nc, bank_a[first], first, wo_codes, wo_scales, e_codes, e_scales)

        interleave(nc.vector.tensor_copy, h_grp, h_raw, 0, HALF)
        interleave(nc.vector.tensor_copy, h_grp, h_raw, HALF, H_SPLIT)
        interleave(nc.scalar.copy, h_grp, h_raw, H_SPLIT, N)
        quantize(nc, h_codes, h_scales, h_grp, 0, HALF)
        quantize(nc, h_codes, h_scales, h_grp, HALF, N)

        for g in order[1:]:
            product(nc, bank_a[g], g, wo_codes, wo_scales, h_codes, h_scales)
        for g in order:
            for cols in (slice(0, HALF), slice(HALF, N)):
                nc.vector.tensor_tensor(out=y[g][:, cols], in0=bank_a[g][:, cols], in1=res_sb[:, g, cols], op=ALU.add)
                nc.sync.dma_start(out=out[g][:, cols], in_=y[g][:, cols])
